import numpy as np
import ml_dtypes


def mxq(x, axis, fmt="e4m3"):
    dtype, down = {"e4m3": (ml_dtypes.float8_e4m3fn, 7), "e5m2": (ml_dtypes.float8_e5m2, 14)}[fmt]
    v = np.moveaxis(np.asarray(x, np.float32).astype(ml_dtypes.bfloat16).astype(np.float64), axis, -1)
    blocks = v.reshape(v.shape[:-1] + (-1, 32))
    amax = np.abs(blocks).max(-1, keepdims=True)
    byte = np.maximum(np.where(amax > 0, np.frexp(amax)[1] - 1 + 127, 0) - down, 1)
    scale = np.exp2(byte - 127.0)
    codes = (blocks / scale).astype(np.float32).astype(dtype).astype(np.float64)
    return np.moveaxis((codes * scale).reshape(v.shape), -1, axis)


WIDE = False


def mx_kscale(k):
    if not WIDE:
        return np.ones(k)
    levels = np.array([10, -10, 5, -5, 0])
    if k % 512:
        return np.exp2(np.random.permutation(np.resize(levels, k // 32))).repeat(32)
    a = np.empty((k // 512, 16))
    for p in range(k // 512):
        a[p, :8] = np.random.permutation(np.resize(levels, 8))
        for g in range(8):
            far = levels[np.abs(levels - a[p, g]) >= 10]
            a[p, g + 8] = far[np.random.randint(len(far))]
    return np.exp2(a.ravel()).repeat(32)


BF16 = ml_dtypes.bfloat16


def bf(x):
    return np.asarray(x, np.float32).astype(BF16)


def f64(x):
    return np.asarray(x).astype(np.float64)


N, D, H, O = 4096, 1024, 512, 512

BETA = 0.5


def nudged_states(a, f, beta):
    hp = np.tanh(a + beta * f)
    hm = np.tanh(a - beta * f)
    return hp, hm


def draw0():
    s, u, t = mx_kscale(D), mx_kscale(O), mx_kscale(N)
    return {"x": bf(np.random.standard_normal((N, D))),
            "p": bf((1.0 + 0.1 * np.random.standard_normal(D)) * s),
            "w1": bf(np.random.standard_normal((D, H)) / np.sqrt(D) / s[:, None]),
            "e": bf(np.random.standard_normal((N, O)) * u[None, :]),
            "w2": bf(np.random.standard_normal((H, O)) / np.sqrt(O) / u[None, :]),
            "r": bf((1.0 + 0.1 * np.random.standard_normal(N)) * t),
            "g": bf((1.0 + 0.1 * np.random.standard_normal(N)) / t)}


def core(x, p, w1, e, w2, r, g):
    x, p, w1, e, w2, r, g = f64(x), f64(p), f64(w1), f64(e), f64(w2), f64(r), f64(g)
    n = x.shape[0]
    a = mxq(x * p[None, :], 1, "e4m3") @ mxq(w1, 0, "e4m3")
    f = mxq(e, 1, "e4m3") @ mxq(w2, 1, "e4m3").T
    hp, hm = nudged_states(a, f, BETA)
    d = (hp - hm) * g[:, None] / (2.0 * BETA * np.sqrt(n))
    xr = x * r[:, None]
    return mxq(xr, 0, "e4m3").T @ mxq(d, 0, "e4m3")


def e4m3fn_bytes(y):
    return np.clip(np.asarray(y, np.float64), -448.0, 448.0).astype(np.float32).astype(ml_dtypes.float8_e4m3fn).view(np.uint8)


def e4m3fn_values(b):
    return np.asarray(b, np.uint8).view(ml_dtypes.float8_e4m3fn).astype(np.float64)


def setup_inputs():
    d = draw0()
    x0 = np.asarray(d['e']).astype(np.float64)
    s = (np.max(np.abs(x0), axis=(0,), keepdims=True) / 448.0).astype(np.float32)
    out = {}
    for k, v in d.items():
        if k == 'e':
            out['e_bytes'] = e4m3fn_bytes(x0 / s.astype(np.float64))
            out['e_scale'] = s
        else:
            out[k] = v
    return out


def reference(x, p, w1, e_bytes, e_scale, w2, r, g):
    return core(x, p, w1, e4m3fn_values(e_bytes) * e_scale.astype(np.float64), w2, r, g)

@@ -1,0 +1,455 @@
+from contextlib import ExitStack
+
+import concourse.mybir as mybir
+from concourse.masks import make_identity
+
+F32 = mybir.dt.float32
+BF16 = mybir.dt.bfloat16
+U32 = mybir.dt.uint32
+U8 = mybir.dt.uint8
+FP8 = mybir.dt.float8_e4m3fn
+FP8X4 = mybir.dt.float8_e4m3fn_x4
+MULT = mybir.AluOpType.mult
+SUB = mybir.AluOpType.subtract
+TANH = mybir.ActivationFunctionType.Tanh
+
+N, D, H, O = 4096, 1024, 512, 512
+FLOPS = 2 * N * D * H + 2 * N * O * H + 2 * N * D * H
+P = 128
+G = 8
+T = 4
+OPEN = 3
+TR = 2
+UB = 8 - OPEN - TR
+SHIFT = 4
+LAG = 2
+CH = {(5, 0): (3, 4), (5, 2): (4, 4), (6, 0): (5, 5), (6, 1): (6, 5), (6, 2): (7, 5)}
+QX = 3
+QD = 2
+LAG7 = 1
+HB = 4
+SG = (1, 3, 5)
+IL_COLS = 128
+IL_V = 0
+
+
+def tile_centredequilibriumpropupdate_t_kernel(tc, x, p, w1, e_bytes, e_scale, w2, r, g, out):
+    nc = tc.nc
+    x_v = x.rearrange("(g p t) d -> g p t d", p=P, t=T)
+    e_v = e_bytes.rearrange("(g p t) o -> g p (t o)", p=P, t=T)
+    w1_v = w1.rearrange("(c p t) h -> p c t h", p=P, t=T)
+    w2_v = w2.rearrange("(a p) o -> p a o", p=P)
+    with ExitStack() as ctx:
+        keep = ctx.enter_context(tc.tile_pool(name="keep", bufs=1))
+        work = ctx.enter_context(tc.tile_pool(name="work", bufs=2))
+        psum = ctx.enter_context(tc.psum_pool(name="psum", bufs=1))
+
+        def codes(n, name):
+            c = keep.tile([P, n], U32, name=name + "_c", align_bytes=64)
+            s = keep.tile([P, n], U8, name=name + "_s", align_bytes=64)
+            return c, s
+
+        def codes_w(n, tag, bufs):
+            c = work.tile([P, n], U32, tag=tag + "_c", bufs=bufs, align_bytes=64, name=tag + "_c")
+            s = work.tile([P, n], U8, tag=tag + "_s", bufs=bufs, align_bytes=64, name=tag + "_s")
+            return c, s
+
+        def quant(cs, src):
+            nc.vector.quantize_mx(out=cs[0][:].bitcast(FP8X4), scales=cs[1][:], in_=src)
+
+        xs, ebs, ebf, xrs, xri, xt, et, xq, eq = {}, {}, {}, {}, {}, {}, {}, {}, {}
+        hps, dif, dil, dq, xrq, bank, acc, dsc = {}, {}, {}, {}, {}, {}, {}, {}
+
+        if N:
+            warm = keep.tile([P, 1], F32, name="warm")
+            nc.vector.memset(warm[:], 0.0)
+            warm2 = keep.tile([P, 1], F32, name="warm2")
+            nc.scalar.activation(out=warm2[:], in_=warm[:], func=TANH)
+            ident = keep.tile([P, P], F32, name="ident")
+            make_identity(nc, ident[:])
+
+            def load_x(i):
+                xs[i] = work.tile([P, T, D], BF16, tag="x", bufs=3, align_bytes=64, name="x_raw")
+                for h in range(2):
+                    nc.sync.dma_start(out=xs[i][:, 2 * h : 2 * h + 2, :], in_=x_v[i][:, 2 * h : 2 * h + 2, :])
+
+            def load_e(i):
+                ebs[i] = work.tile([P, T * O], U8, tag="ebytes", bufs=3, align_bytes=64, name="e_raw")
+                nc.sync.dma_start(out=ebs[i][:], in_=e_v[i])
+
+            def load_w1(c):
+                w = work.tile([P, T, H], BF16, tag="dif", bufs=2, align_bytes=64, name="w1_raw")
+                nc.sync.dma_start(out=w[:], in_=w1_v[:, c])
+                w1_raw.append(w)
+
+            def load_x0(h):
+                if h == 0:
+                    xs[0] = work.tile([P, T, D], BF16, tag="x", bufs=3, align_bytes=64, name="x_raw")
+                nc.sync.dma_start(out=xs[0][:, 2 * h : 2 * h + 2, :], in_=x_v[0][:, 2 * h : 2 * h + 2, :])
+
+            w1_raw = []
+            load_e(0)
+            es = keep.tile([P, O], F32, name="es", align_bytes=64)
+            nc.sync.dma_start(out=es[:], in_=e_scale.rearrange("o k -> (o k)").partition_broadcast(P))
+            load_x0(0)
+            p_sb = keep.tile([P, 2, T], BF16, name="p_sb")
+            nc.scalar.dma_start(out=p_sb[:], in_=p.rearrange("(c p t) -> p c t", p=P, t=T))
+            w2_raw = work.tile([P, T, O], BF16, tag="et", bufs=2, align_bytes=64, name="w2_raw")
+            nc.sync.dma_start(out=w2_raw[:], in_=w2_v)
+            load_w1(0)
+            load_w1(1)
+            load_x0(1)
+            r_sb = keep.tile([P, G, T], BF16, name="r_sb")
+            nc.scalar.dma_start(out=r_sb[:], in_=r.rearrange("(g p t) -> p g t", p=P, t=T))
+            g_sb = keep.tile([P, G, T], BF16, name="g_sb")
+            nc.scalar.dma_start(out=g_sb[:], in_=g.rearrange("(g p t) -> p g t", p=P, t=T))
+            load_x(1)
+            load_e(1)
+            load_x(2)
+            load_e(2)
+
+            g64 = keep.tile([P, G, T], F32, name="g64")
+            def scale_xr(i, ts=range(T)):
+                if i not in xrs:
+                    xrs[i] = work.tile([P, T, D], BF16, tag="xrs", bufs=2, align_bytes=64, name="xrs")
+                for t in ts:
+                    nc.vector.tensor_scalar(out=xrs[i][:, t, :], in0=xs[i][:, t, :], scalar1=r_sb[:, i, t : t + 1], scalar2=None, op0=MULT)
+
+            def interleave(eng, dst, src):
+                eng(out=dst.rearrange("p (c i) t -> p c t i", i=4), in_=src.rearrange("p t (c i) -> p c t i", i=4))
+
+            def inter_xr(i, k):
+                if i not in xri:
+                    xri[i] = work.tile([P, D, T], BF16, tag="xri", bufs=2, align_bytes=64, name="xri")
+                cs = slice(k * IL_COLS, (k + 1) * IL_COLS)
+                nblk = D // IL_COLS
+                eng = nc.vector.tensor_copy if k >= nblk - IL_V else nc.scalar.copy
+                interleave(eng, xri[i][:, cs, :], xrs[i][:, :, cs])
+
+            def quant_xr(i):
+                xrq[i] = codes(D, "xrq%d" % i)
+                quant(xrq[i], xri[i][:].rearrange("p d t -> p (d t)"))
+
+            def scale_e(i, ts=range(T)):
+                if i not in ebf:
+                    ebf[i] = work.tile([P, T, O], BF16, tag="ebf", bufs=2, align_bytes=64, name="ebf")
+                for t in ts:
+                    nc.vector.tensor_tensor(out=ebf[i][:, t, :], in0=ebs[i][:, t * O : (t + 1) * O].bitcast(FP8), in1=es[:], op=MULT)
+
+            def transposes(words, t2, key, off):
+                b = psum.tile([P, 2, 2 * P], F32, tag="tr", bufs=TR, name="tr")
+                for a in range(2):
+                    for u in range(2):
+                        nc.tensor.transpose(b[:, u, a * P : (a + 1) * P], words(2 * t2 + a)[:, off + u : off + 2 * P : 2], ident[:])
+                bank[key] = b
+
+            def tr_x(i, k):
+                c, t2 = k // 2, k % 2
+                transposes(lambda t: xs[i][:, t, :].bitcast(F32), t2, ("x", i, k), 256 * c)
+
+            def exit_x(i, k):
+                c, t2 = k // 2, k % 2
+                if (i, c) not in xt:
+                    xt[i, c] = work.tile([P, T * P * 4], BF16, tag="xt", bufs=3, align_bytes=64, name="xt")
+                b = bank[("x", i, k)]
+                nc.vector.tensor_tensor(
+                    out=xt[i, c][:, t2 * 1024 : (t2 + 1) * 1024].rearrange("p (m u e) -> p m u e", u=2, e=2),
+                    in0=b[:].bitcast(BF16).rearrange("p u (m e) -> p m u e", e=2),
+                    in1=p_sb[:, c : c + 1, :].rearrange("p o (u e) -> p o u e", u=2).to_broadcast([P, 256, 2, 2]),
+                    op=MULT,
+                )
+
+            def quant_part(cs, src, part, parts):
+                n = src.shape[1] // parts
+                ws = slice(part * n // 4, (part + 1) * n // 4)
+                nc.vector.quantize_mx(out=cs[0][:, ws].bitcast(FP8X4), scales=cs[1][:, ws], in_=src[:, part * n : (part + 1) * n])
+
+            def quant_x(i, c, part=0, parts=1):
+                if (i, c) not in xq:
+                    xq[i, c] = codes_w(T * P, "xq", 4)
+                quant_part(xq[i, c], xt[i, c][:], part, parts)
+
+            def tr_e(i, t2):
+                transposes(lambda t: ebf[i][:, t, :].bitcast(F32), t2, ("e", i, t2), 0)
+
+            def exit_e(i, t2):
+                if i not in et:
+                    et[i] = work.tile([P, T * P * 4], BF16, tag="et", bufs=2, align_bytes=64, name="et")
+                b = bank[("e", i, t2)]
+                nc.scalar.copy(
+                    out=et[i][:, t2 * 1024 : (t2 + 1) * 1024].bitcast(F32).rearrange("p (m u) -> p m u", u=2),
+                    in_=b[:].rearrange("p u m -> p m u"),
+                )
+
+            def quant_e(i, part=0, parts=1):
+                if i not in eq:
+                    eq[i] = codes_w(T * P, "eq", 2)
+                quant_part(eq[i], et[i][:], part, parts)
+
+            def mx(o, l, r_, cols, start, stop):
+                nc.tensor.matmul_mx(
+                    out=o,
+                    lhsT=l[0][:, cols].bitcast(FP8X4),
+                    lhsT_scale=l[1][:, cols],
+                    rhs=r_[0][:].bitcast(FP8X4),
+                    rhs_scale=r_[1][:],
+                    start=start,
+                    stop=stop,
+                )
+
+            def mm_u(i, t, s):
+                b = psum.tile([P, H], F32, tag="u", bufs=UB, name="u")
+                cols = slice(t * P, (t + 1) * P)
+                mx(b[:], xq[i, 0], w1q[0], cols, True, False)
+                mx(b[:], xq[i, 1], w1q[1], cols, False, False)
+                mx(b[:], eq[i], w2q[s], cols, False, True)
+                bank[("u", i, t, s)] = b
+
+            def tanh(i, t, s):
+                h = work.tile([P, H], F32, tag="h%d" % s, bufs=HB, name="h%d" % s)
+                nc.scalar.activation(out=h[:], in_=bank[("u", i, t, s)][:], func=TANH)
+                hps[i, t, s] = h
+
+            def diff(i, t):
+                if i in SG:
+                    if t == 0:
+                        dsc[i] = work.tile([P, T, H], BF16, tag="dsc", bufs=2, align_bytes=64, name="dsc")
+                    nc.vector.scalar_tensor_tensor(out=dsc[i][:, t, :], in0=hps[i, t, 0][:], scalar=g64[:, i, t : t + 1], in1=hps[i, t, 1][:], op0=MULT, op1=SUB)
+                    return
+                if i not in dif:
+                    dif[i] = work.tile([P, T, H], F32, tag="dif", bufs=2, align_bytes=64, name="dif")
+                nc.vector.tensor_tensor(out=dif[i][:, t, :], in0=hps[i, t, 0][:], in1=hps[i, t, 1][:], op=SUB)
+
+            def gmul(i, h):
+                if i not in dil:
+                    dil[i] = work.tile([P, H, T], BF16, tag="dil", bufs=2, align_bytes=64, name="dil")
+                hs = slice(h * 256, (h + 1) * 256)
+                nc.vector.tensor_tensor(
+                    out=dil[i][:, hs, :],
+                    in0=dif[i][:, :, hs].rearrange("p t h -> p h t"),
+                    in1=g64[:, i : i + 1, :].to_broadcast([P, 256, T]),
+                    op=MULT,
+                )
+
+            def quant_d(i, part=0, parts=1):
+                if i not in dq:
+                    dq[i] = codes(H, "dq%d" % i)
+                quant_part(dq[i], dil[i][:].rearrange("p h t -> p (h t)"), part, parts)
+
+            def gscale(i, t):
+                h = hps[i, t, 1]
+                nc.scalar.activation(out=h[:], in_=h[:], func=mybir.ActivationFunctionType.Copy, scale=g64[:, i, t : t + 1])
+
+            def gil(i, h):
+                if i not in dil:
+                    dil[i] = work.tile([P, H, T], BF16, tag="dil", bufs=2, align_bytes=64, name="dil")
+                hs = slice(h * 256, (h + 1) * 256)
+                interleave(nc.vector.tensor_copy, dil[i][:, hs, :], dsc[i][:, :, hs])
+
+            def mm_acc(i, m, tag=None):
+                if m not in acc:
+                    if m < OPEN:
+                        acc[m] = psum.tile([P, H], F32, tag="acc%d" % m, bufs=1, name="acc")
+                    elif m < OPEN + TR:
+                        acc[m] = psum.tile([P, H], F32, tag="tr", bufs=TR, name="tr")
+                    else:
+                        acc[m] = psum.tile([P, H], F32, tag="u", bufs=UB, name="u")
+                mx(acc[m][:], xrq[i], dq[i], slice(m * P, (m + 1) * P), i == first.get(m, 0), i == G - 1)
+
+            part = {}
+            outs = []
+
+            def chunk(m, k0):
+                b = psum.tile([P, H], F32, tag="u", bufs=UB, name="u")
+                for k in range(k0):
+                    mx(b[:], xrq[k], dq[k], slice(m * P, (m + 1) * P), k == 0, k == k0 - 1)
+                part[m] = work.tile([P, H], F32, tag="part", bufs=5, name="part")
+                nc.scalar.copy(out=part[m][:], in_=b[:])
+                first[m] = k0
+
+            first = {}
+
+            def finish(m):
+                if m % 4 == 0:
+                    outs.append(work.tile([P, 4, H], F32, tag="xrs", bufs=2, align_bytes=64, name="o"))
+                o = outs[m // 4][:, m % 4, :]
+                if m in part:
+                    nc.vector.tensor_tensor(out=o, in0=acc[m][:], in1=part[m][:], op=mybir.AluOpType.add)
+                elif m % 2 == 0 or len(part) > 3:
+                    nc.scalar.copy(out=o, in_=acc[m][:])
+                else:
+                    nc.vector.tensor_copy(out=o, in_=acc[m][:])
+                nc.sync.dma_start(out=out[m * P : (m + 1) * P, :], in_=o)
+
+            nblk = D // IL_COLS
+            ilq = [(i, k) for i in range(G) for k in range(nblk)]
+            ilpos = [0]
+
+            def il_upto(pos):
+                while ilpos[0] < min(pos, len(ilq)):
+                    inter_xr(*ilq[ilpos[0]])
+                    ilpos[0] += 1
+
+            w2t = work.tile([P, T * P * 4], BF16, tag="ebf", bufs=2, align_bytes=64, name="w2t")
+            w1i = [work.tile([P, H, T], BF16, tag="xri", bufs=2, align_bytes=64, name="w1i") for c in range(2)]
+
+            def il_w1(eng, c, k):
+                interleave(eng, w1i[c][:, k * 128 : (k + 1) * 128, :], w1_raw[c][:, :, k * 128 : (k + 1) * 128])
+
+            w2h = [None, None]
+            w2q = [None, None]
+
+            def prep_w2(s):
+                w2h[s] = work.tile([P, T * P * 4], BF16, tag="dil", bufs=2, align_bytes=64, name="w2h")
+                nc.vector.tensor_scalar(out=w2h[s][:], in0=w2t[:], scalar1=0.5 if s == 0 else -0.5, scalar2=None, op0=MULT)
+
+            def quant_w2(s):
+                w2q[s] = codes(H, "w2q%d" % s)
+                quant(w2q[s], w2h[s][:])
+
+            scale_e(0, range(0, 2))
+            tr_e(0, 0)
+            exit_e(0, 0)
+            tr_x(0, 0)
+            exit_x(0, 0)
+            tr_x(0, 2)
+            exit_x(0, 2)
+            for t2 in range(2):
+                transposes(lambda t: w2_raw[:, t, :].bitcast(F32), t2, ("w2", t2), 0)
+                nc.scalar.copy(
+                    out=w2t[:, t2 * 1024 : (t2 + 1) * 1024].bitcast(F32).rearrange("p (m u) -> p m u", u=2),
+                    in_=bank[("w2", t2)][:].rearrange("p u m -> p m u"),
+                )
+            quant_e(0, 0, 2)
+            quant_x(0, 0, 0, 2)
+            quant_x(0, 1, 0, 2)
+            nc.vector.tensor_scalar(out=g64[:], in0=g_sb[:], scalar1=1.0 / 64.0, scalar2=None, op0=MULT)
+            scale_e(0, range(2, 4))
+            prep_w2(0)
+            prep_w2(1)
+            for c in range(2):
+                il_w1(nc.scalar.copy, c, 0)
+                il_w1(nc.scalar.copy, c, 1)
+                il_w1(nc.vector.tensor_copy, c, 2)
+                il_w1(nc.vector.tensor_copy, c, 3)
+            quant_w2(0)
+            quant_w2(1)
+            w1q = [codes(H, "w1q%d" % c) for c in range(2)]
+            for c in range(2):
+                quant(w1q[c], w1i[c][:].rearrange("p h t -> p (h t)"))
+            tr_e(0, 1)
+            exit_e(0, 1)
+            tr_x(0, 1)
+            tr_x(0, 3)
+            scale_xr(0)
+            exit_x(0, 1)
+            exit_x(0, 3)
+            quant_e(0, 1, 2)
+            quant_x(0, 0, 1, 2)
+            quant_x(0, 1, 1, 2)
+            scale_e(1)
+
+            def gm(i, h):
+                if i in SG:
+                    gil(i, h)
+                else:
+                    gmul(i, h)
+
+            dpos = [0]
+
+            def diffs_upto(pos):
+                while dpos[0] < pos:
+                    diff(dpos[0] // T, dpos[0] % T)
+                    dpos[0] += 1
+
+            tr_x(1, 0)
+            tr_x(1, 1)
+            for i in range(G):
+                n = i + 1
+                pr = i - 1
+                if i + 3 < G:
+                    load_x(i + 3)
+                    load_e(i + 3)
+                for t in range(T):
+                    mm_u(i, t, 0)
+                    mm_u(i, t, 1)
+                    if (i, t) in CH:
+                        chunk(*CH[i, t])
+                    if n < G:
+                        if t == 0:
+                            exit_x(n, 0)
+                            exit_x(n, 1)
+                        elif t == 1:
+                            exit_x(n, 2)
+                            exit_x(n, 3)
+                        elif t == 2:
+                            exit_e(n, 0)
+                            exit_e(n, 1)
+                        if t == 0:
+                            tr_x(n, 2)
+                            tr_x(n, 3)
+                        elif t == 1:
+                            tr_e(n, 0)
+                            tr_e(n, 1)
+                        elif t == 3 and n + 1 < G:
+                            tr_x(n + 1, 0)
+                            tr_x(n + 1, 1)
+                    pos = 8 * i + 2 * t + SHIFT
+                    tanh(i, t, 0)
+                    il_upto(pos + 1)
+                    tanh(i, t, 1)
+                    if i in SG:
+                        gscale(i, t)
+                    il_upto(pos + 2)
+                    if t == QX:
+                        for q in range(n):
+                            if q not in xrq and ilpos[0] - QD >= 8 * (q + 1):
+                                quant_xr(q)
+                    lag = LAG if n < G else LAG7
+                    dp = 4 * i + t - lag + 1
+                    if t == 0:
+                        if n < G:
+                            scale_xr(n)
+                        diffs_upto(dp)
+                    elif t == 1:
+                        if n < G:
+                            quant_x(n, 0)
+                        diffs_upto(dp)
+                    elif t == 2:
+                        if pr >= 0:
+                            gm(pr, 0)
+                        if n < G:
+                            quant_x(n, 1)
+                        if pr >= 0:
+                            gm(pr, 1)
+                        diffs_upto(dp)
+                    else:
+                        if n < G:
+                            quant_e(n)
+                        if pr >= 0:
+                            quant_d(pr)
+                        if n + 1 < G:
+                            scale_e(n + 1)
+                        diffs_upto(dp)
+                        if pr >= 0:
+                            for m in range(OPEN if n < G else OPEN + TR):
+                                mm_acc(pr, m)
+                    if n == G and t < 3:
+                        for m in range(OPEN, OPEN + TR):
+                            for k in range(first.get(m, 0), 6):
+                                if k * 3 // 6 == t or (t == 0 and k * 3 // 6 < t):
+                                    mm_acc(k, m)
+            last = G - 1
+            if last not in xrq:
+                quant_xr(last)
+            for k in range(7):
+                for m in range(OPEN + TR, 8):
+                    if k >= first.get(m, 0):
+                        mm_acc(k, m)
+            diffs_upto(4 * G)
+            gm(last, 0)
+            gm(last, 1)
+            quant_d(last)
+            for m in range(8):
+                mm_acc(last, m)
+                finish(m)

@@ -28,7 +28,7 @@ QX = 3
 QD = 2
 LAG7 = 1
 HB = 4
-SG = (1, 3, 5)
+SG = (1, 3, 5, 7)
 IL_COLS = 128
 IL_V = 0
 
@@ -88,27 +88,43 @@ def tile_centredequilibriumpropupdate_t_kernel(tc, x, p, w1, e_bytes, e_scale, w
                 nc.sync.dma_start(out=xs[0][:, 2 * h : 2 * h + 2, :], in_=x_v[0][:, 2 * h : 2 * h + 2, :])
 
             w1_raw = []
-            load_e(0)
-            es = keep.tile([P, O], F32, name="es", align_bytes=64)
-            nc.sync.dma_start(out=es[:], in_=e_scale.rearrange("o k -> (o k)").partition_broadcast(P))
+            vecs = keep.tile([P, 256], F32, name="vecs", align_bytes=64)
+            nc.vector.memset(vecs[:], 0.0)
+            vb = vecs[:].bitcast(BF16)
+            nc.scalar.dma_start(out=vecs[18:20, :], in_=e_scale.rearrange("o (a w) -> (o a) w", a=2))
+            nc.scalar.dma_start(out=vb[16:18, :], in_=p.rearrange("(c w) -> c w", c=2))
+            nc.scalar.dma_start(out=vb[0:8, :], in_=r.rearrange("(c w) -> c w", c=G))
+            nc.scalar.dma_start(out=vb[8:16, :], in_=g.rearrange("(c w) -> c w", c=G))
             load_x0(0)
-            p_sb = keep.tile([P, 2, T], BF16, name="p_sb")
-            nc.scalar.dma_start(out=p_sb[:], in_=p.rearrange("(c p t) -> p c t", p=P, t=T))
+            load_e(0)
             w2_raw = work.tile([P, T, O], BF16, tag="et", bufs=2, align_bytes=64, name="w2_raw")
             nc.sync.dma_start(out=w2_raw[:], in_=w2_v)
             load_w1(0)
             load_w1(1)
             load_x0(1)
-            r_sb = keep.tile([P, G, T], BF16, name="r_sb")
-            nc.scalar.dma_start(out=r_sb[:], in_=r.rearrange("(g p t) -> p g t", p=P, t=T))
-            g_sb = keep.tile([P, G, T], BF16, name="g_sb")
-            nc.scalar.dma_start(out=g_sb[:], in_=g.rearrange("(g p t) -> p g t", p=P, t=T))
             load_x(1)
             load_e(1)
             load_x(2)
             load_e(2)
 
+            vp = psum.tile([P, 2, P], F32, tag="tr", bufs=TR, name="tr")
+            for u in range(2):
+                nc.tensor.transpose(vp[:, u, :], vecs[:, u::2], ident[:])
+            cols = keep.tile([P, 20, 2], F32, name="cols", align_bytes=64)
+            nc.scalar.copy(out=cols[:], in_=vp[:, :, 0:20].rearrange("p u c -> p c u"))
+            colb = cols[:].rearrange("p c u -> p (c u)").bitcast(BF16).rearrange("p (c t) -> p c t", t=T)
+            r_sb = colb[:, 0:8, :]
+            p_sb = colb[:, 16:18, :]
+            esp = psum.tile([P, 2, 2, P], F32, tag="tr", bufs=TR, name="tr")
+            for h in range(2):
+                for u in range(2):
+                    nc.tensor.transpose(esp[:, h, u, :], cols[:, 18 + h, u : u + 1].to_broadcast([P, P]), ident[:])
+            es = keep.tile([P, T, O], F32, name="es", align_bytes=64)
+            for t in range(T):
+                nc.scalar.mul(out=es[:, t, :].rearrange("p (h w u) -> p h w u", h=2, u=2), in_=esp[:].rearrange("p h u w -> p h w u"), mul=0.5)
             g64 = keep.tile([P, G, T], F32, name="g64")
+            nc.vector.tensor_scalar(out=g64[:], in0=colb[:, 8:16, :], scalar1=1.0 / 64.0, scalar2=None, op0=MULT)
+
             def scale_xr(i, ts=range(T)):
                 if i not in xrs:
                     xrs[i] = work.tile([P, T, D], BF16, tag="xrs", bufs=2, align_bytes=64, name="xrs")
@@ -133,8 +149,13 @@ def tile_centredequilibriumpropupdate_t_kernel(tc, x, p, w1, e_bytes, e_scale, w
             def scale_e(i, ts=range(T)):
                 if i not in ebf:
                     ebf[i] = work.tile([P, T, O], BF16, tag="ebf", bufs=2, align_bytes=64, name="ebf")
-                for t in ts:
-                    nc.vector.tensor_tensor(out=ebf[i][:, t, :], in0=ebs[i][:, t * O : (t + 1) * O].bitcast(FP8), in1=es[:], op=MULT)
+                sl = slice(ts[0] * O, (ts[-1] + 1) * O)
+                nc.vector.tensor_tensor(
+                    out=ebf[i][:].rearrange("p t o -> p (t o)")[:, sl],
+                    in0=ebs[i][:, sl].bitcast(FP8),
+                    in1=es[:].rearrange("p t o -> p (t o)")[:, sl],
+                    op=MULT,
+                )
 
             def transposes(words, t2, key, off):
                 b = psum.tile([P, 2, 2 * P], F32, tag="tr", bufs=TR, name="tr")
@@ -206,19 +227,20 @@ def tile_centredequilibriumpropupdate_t_kernel(tc, x, p, w1, e_bytes, e_scale, w
                 bank[("u", i, t, s)] = b
 
             def tanh(i, t, s):
-                h = work.tile([P, H], F32, tag="h%d" % s, bufs=HB, name="h%d" % s)
-                nc.scalar.activation(out=h[:], in_=bank[("u", i, t, s)][:], func=TANH)
-                hps[i, t, s] = h
+                if (i, t // 2, s) not in hps:
+                    hps[i, t // 2, s] = work.tile([P, 2, H], F32, tag="h%d" % s, bufs=2, align_bytes=64, name="h%d" % s)
+                nc.scalar.activation(out=hps[i, t // 2, s][:, t % 2, :], in_=bank[("u", i, t, s)][:], func=TANH)
 
             def diff(i, t):
                 if i in SG:
                     if t == 0:
-                        dsc[i] = work.tile([P, T, H], BF16, tag="dsc", bufs=2, align_bytes=64, name="dsc")
-                    nc.vector.scalar_tensor_tensor(out=dsc[i][:, t, :], in0=hps[i, t, 0][:], scalar=g64[:, i, t : t + 1], in1=hps[i, t, 1][:], op0=MULT, op1=SUB)
+                        dsc[i] = work.tile([P, T, H], BF16, tag="dif", bufs=2, align_bytes=64, name="dsc")
+                    nc.vector.scalar_tensor_tensor(out=dsc[i][:, t, :], in0=hps[i, t // 2, 0][:, t % 2, :], scalar=g64[:, i, t : t + 1], in1=hps[i, t // 2, 1][:, t % 2, :], op0=MULT, op1=SUB)
                     return
                 if i not in dif:
                     dif[i] = work.tile([P, T, H], F32, tag="dif", bufs=2, align_bytes=64, name="dif")
-                nc.vector.tensor_tensor(out=dif[i][:, t, :], in0=hps[i, t, 0][:], in1=hps[i, t, 1][:], op=SUB)
+                if t % 2 == 1:
+                    nc.vector.tensor_tensor(out=dif[i][:, t - 1 : t + 1, :], in0=hps[i, t // 2, 0][:], in1=hps[i, t // 2, 1][:], op=SUB)
 
             def gmul(i, h):
                 if i not in dil:
@@ -237,8 +259,8 @@ def tile_centredequilibriumpropupdate_t_kernel(tc, x, p, w1, e_bytes, e_scale, w
                 quant_part(dq[i], dil[i][:].rearrange("p h t -> p (h t)"), part, parts)
 
             def gscale(i, t):
-                h = hps[i, t, 1]
-                nc.scalar.activation(out=h[:], in_=h[:], func=mybir.ActivationFunctionType.Copy, scale=g64[:, i, t : t + 1])
+                h = hps[i, t // 2, 1][:, t % 2, :]
+                nc.scalar.activation(out=h, in_=h, func=mybir.ActivationFunctionType.Copy, scale=g64[:, i, t : t + 1])
 
             def gil(i, h):
                 if i not in dil:
@@ -300,20 +322,22 @@ def tile_centredequilibriumpropupdate_t_kernel(tc, x, p, w1, e_bytes, e_scale, w
             w2q = [None, None]
 
             def prep_w2(s):
-                w2h[s] = work.tile([P, T * P * 4], BF16, tag="dil", bufs=2, align_bytes=64, name="w2h")
-                nc.vector.tensor_scalar(out=w2h[s][:], in0=w2t[:], scalar1=0.5 if s == 0 else -0.5, scalar2=None, op0=MULT)
+                w2h[s] = w2t
+                if s == 1:
+                    w2h[s] = work.tile([P, T * P * 4], BF16, tag="dil", bufs=2, align_bytes=64, name="w2h")
+                    nc.vector.tensor_scalar(out=w2h[s][:], in0=w2t[:], scalar1=-1.0, scalar2=None, op0=MULT)
 
             def quant_w2(s):
                 w2q[s] = codes(H, "w2q%d" % s)
                 quant(w2q[s], w2h[s][:])
 
-            scale_e(0, range(0, 2))
-            tr_e(0, 0)
-            exit_e(0, 0)
             tr_x(0, 0)
             exit_x(0, 0)
             tr_x(0, 2)
             exit_x(0, 2)
+            scale_e(0, range(0, 2))
+            tr_e(0, 0)
+            exit_e(0, 0)
             for t2 in range(2):
                 transposes(lambda t: w2_raw[:, t, :].bitcast(F32), t2, ("w2", t2), 0)
                 nc.scalar.copy(
@@ -323,7 +347,6 @@ def tile_centredequilibriumpropupdate_t_kernel(tc, x, p, w1, e_bytes, e_scale, w
             quant_e(0, 0, 2)
             quant_x(0, 0, 0, 2)
             quant_x(0, 1, 0, 2)
-            nc.vector.tensor_scalar(out=g64[:], in0=g_sb[:], scalar1=1.0 / 64.0, scalar2=None, op0=MULT)
             scale_e(0, range(2, 4))
             prep_w2(0)
             prep_w2(1)
@@ -371,8 +394,9 @@ def tile_centredequilibriumpropupdate_t_kernel(tc, x, p, w1, e_bytes, e_scale, w
                     load_x(i + 3)
                     load_e(i + 3)
                 for t in range(T):
-                    mm_u(i, t, 0)
-                    mm_u(i, t, 1)
+                    sides = (1, 0) if i in SG else (0, 1)
+                    for s in sides:
+                        mm_u(i, t, s)
                     if (i, t) in CH:
                         chunk(*CH[i, t])
                     if n < G:
@@ -395,11 +419,11 @@ def tile_centredequilibriumpropupdate_t_kernel(tc, x, p, w1, e_bytes, e_scale, w
                             tr_x(n + 1, 0)
                             tr_x(n + 1, 1)
                     pos = 8 * i + 2 * t + SHIFT
-                    tanh(i, t, 0)
-                    il_upto(pos + 1)
-                    tanh(i, t, 1)
+                    tanh(i, t, sides[0])
                     if i in SG:
                         gscale(i, t)
+                    il_upto(pos + 1)
+                    tanh(i, t, sides[1])
                     il_upto(pos + 2)
                     if t == QX:
                         for q in range(n):
@@ -432,24 +456,19 @@ def tile_centredequilibriumpropupdate_t_kernel(tc, x, p, w1, e_bytes, e_scale, w
                             scale_e(n + 1)
                         diffs_upto(dp)
                         if pr >= 0:
-                            for m in range(OPEN if n < G else OPEN + TR):
+                            for m in range(OPEN):
                                 mm_acc(pr, m)
-                    if n == G and t < 3:
-                        for m in range(OPEN, OPEN + TR):
-                            for k in range(first.get(m, 0), 6):
-                                if k * 3 // 6 == t or (t == 0 and k * 3 // 6 < t):
-                                    mm_acc(k, m)
             last = G - 1
             if last not in xrq:
                 quant_xr(last)
-            for k in range(7):
-                for m in range(OPEN + TR, 8):
+            for m in range(OPEN, 8):
+                for k in range(7):
                     if k >= first.get(m, 0):
                         mm_acc(k, m)
             diffs_upto(4 * G)
-            gm(last, 0)
-            gm(last, 1)
-            quant_d(last)
+            for h in range(2):
+                gm(last, h)
+                quant_d(last, h, 2)
             for m in range(8):
                 mm_acc(last, m)
                 finish(m)

from contextlib import ExitStack

import concourse.mybir as mybir
from concourse.masks import make_identity

F32 = mybir.dt.float32
BF16 = mybir.dt.bfloat16
U32 = mybir.dt.uint32
U8 = mybir.dt.uint8
FP8 = mybir.dt.float8_e4m3fn
FP8X4 = mybir.dt.float8_e4m3fn_x4
MULT = mybir.AluOpType.mult
SUB = mybir.AluOpType.subtract
TANH = mybir.ActivationFunctionType.Tanh

N, D, H, O = 4096, 1024, 512, 512
FLOPS = 2 * N * D * H + 2 * N * O * H + 2 * N * D * H
P = 128
G = 8
T = 4
OPEN = 3
TR = 2
UB = 8 - OPEN - TR
SHIFT = 4
LAG = 2
CH = {(5, 0): (3, 4), (5, 2): (4, 4), (6, 0): (5, 5), (6, 1): (6, 5), (6, 2): (7, 5)}
QX = 3
QD = 2
LAG7 = 1
HB = 4
SG = (1, 3, 5, 7)
IL_COLS = 128
IL_V = 0


def tile_centredequilibriumpropupdate_t_kernel(tc, x, p, w1, e_bytes, e_scale, w2, r, g, out):
    nc = tc.nc
    x_v = x.rearrange("(g p t) d -> g p t d", p=P, t=T)
    e_v = e_bytes.rearrange("(g p t) o -> g p (t o)", p=P, t=T)
    w1_v = w1.rearrange("(c p t) h -> p c t h", p=P, t=T)
    w2_v = w2.rearrange("(a p) o -> p a o", p=P)
    with ExitStack() as ctx:
        keep = ctx.enter_context(tc.tile_pool(name="keep", bufs=1))
        work = ctx.enter_context(tc.tile_pool(name="work", bufs=2))
        psum = ctx.enter_context(tc.psum_pool(name="psum", bufs=1))

        def codes(n, name):
            c = keep.tile([P, n], U32, name=name + "_c", align_bytes=64)
            s = keep.tile([P, n], U8, name=name + "_s", align_bytes=64)
            return c, s

        def codes_w(n, tag, bufs):
            c = work.tile([P, n], U32, tag=tag + "_c", bufs=bufs, align_bytes=64, name=tag + "_c")
            s = work.tile([P, n], U8, tag=tag + "_s", bufs=bufs, align_bytes=64, name=tag + "_s")
            return c, s

        def quant(cs, src):
            nc.vector.quantize_mx(out=cs[0][:].bitcast(FP8X4), scales=cs[1][:], in_=src)

        xs, ebs, ebf, xrs, xri, xt, et, xq, eq = {}, {}, {}, {}, {}, {}, {}, {}, {}
        hps, dif, dil, dq, xrq, bank, acc, dsc = {}, {}, {}, {}, {}, {}, {}, {}

        if N:
            warm = keep.tile([P, 1], F32, name="warm")
            nc.vector.memset(warm[:], 0.0)
            warm2 = keep.tile([P, 1], F32, name="warm2")
            nc.scalar.activation(out=warm2[:], in_=warm[:], func=TANH)
            ident = keep.tile([P, P], F32, name="ident")
            make_identity(nc, ident[:])

            def load_x(i):
                xs[i] = work.tile([P, T, D], BF16, tag="x", bufs=3, align_bytes=64, name="x_raw")
                for h in range(2):
                    nc.sync.dma_start(out=xs[i][:, 2 * h : 2 * h + 2, :], in_=x_v[i][:, 2 * h : 2 * h + 2, :])

            def load_e(i):
                ebs[i] = work.tile([P, T * O], U8, tag="ebytes", bufs=3, align_bytes=64, name="e_raw")
                nc.sync.dma_start(out=ebs[i][:], in_=e_v[i])

            def load_w1(c):
                w = work.tile([P, T, H], BF16, tag="dif", bufs=2, align_bytes=64, name="w1_raw")
                nc.sync.dma_start(out=w[:], in_=w1_v[:, c])
                w1_raw.append(w)

            def load_x0(h):
                if h == 0:
                    xs[0] = work.tile([P, T, D], BF16, tag="x", bufs=3, align_bytes=64, name="x_raw")
                nc.sync.dma_start(out=xs[0][:, 2 * h : 2 * h + 2, :], in_=x_v[0][:, 2 * h : 2 * h + 2, :])

            w1_raw = []
            vecs = keep.tile([P, 256], F32, name="vecs", align_bytes=64)
            nc.vector.memset(vecs[:], 0.0)
            vb = vecs[:].bitcast(BF16)
            nc.scalar.dma_start(out=vecs[18:20, :], in_=e_scale.rearrange("o (a w) -> (o a) w", a=2))
            nc.scalar.dma_start(out=vb[16:18, :], in_=p.rearrange("(c w) -> c w", c=2))
            nc.scalar.dma_start(out=vb[0:8, :], in_=r.rearrange("(c w) -> c w", c=G))
            nc.scalar.dma_start(out=vb[8:16, :], in_=g.rearrange("(c w) -> c w", c=G))
            load_x0(0)
            load_e(0)
            w2_raw = work.tile([P, T, O], BF16, tag="et", bufs=2, align_bytes=64, name="w2_raw")
            nc.sync.dma_start(out=w2_raw[:], in_=w2_v)
            load_w1(0)
            load_w1(1)
            load_x0(1)
            load_x(1)
            load_e(1)
            load_x(2)
            load_e(2)

            vp = psum.tile([P, 2, P], F32, tag="tr", bufs=TR, name="tr")
            for u in range(2):
                nc.tensor.transpose(vp[:, u, :], vecs[:, u::2], ident[:])
            cols = keep.tile([P, 20, 2], F32, name="cols", align_bytes=64)
            nc.scalar.copy(out=cols[:], in_=vp[:, :, 0:20].rearrange("p u c -> p c u"))
            colb = cols[:].rearrange("p c u -> p (c u)").bitcast(BF16).rearrange("p (c t) -> p c t", t=T)
            r_sb = colb[:, 0:8, :]
            p_sb = colb[:, 16:18, :]
            esp = psum.tile([P, 2, 2, P], F32, tag="tr", bufs=TR, name="tr")
            for h in range(2):
                for u in range(2):
                    nc.tensor.transpose(esp[:, h, u, :], cols[:, 18 + h, u : u + 1].to_broadcast([P, P]), ident[:])
            es = keep.tile([P, T, O], F32, name="es", align_bytes=64)
            for t in range(T):
                nc.scalar.mul(out=es[:, t, :].rearrange("p (h w u) -> p h w u", h=2, u=2), in_=esp[:].rearrange("p h u w -> p h w u"), mul=0.5)
            g64 = keep.tile([P, G, T], F32, name="g64")
            nc.vector.tensor_scalar(out=g64[:], in0=colb[:, 8:16, :], scalar1=1.0 / 64.0, scalar2=None, op0=MULT)

            def scale_xr(i, ts=range(T)):
                if i not in xrs:
                    xrs[i] = work.tile([P, T, D], BF16, tag="xrs", bufs=2, align_bytes=64, name="xrs")
                for t in ts:
                    nc.vector.tensor_scalar(out=xrs[i][:, t, :], in0=xs[i][:, t, :], scalar1=r_sb[:, i, t : t + 1], scalar2=None, op0=MULT)

            def interleave(eng, dst, src):
                eng(out=dst.rearrange("p (c i) t -> p c t i", i=4), in_=src.rearrange("p t (c i) -> p c t i", i=4))

            def inter_xr(i, k):
                if i not in xri:
                    xri[i] = work.tile([P, D, T], BF16, tag="xri", bufs=2, align_bytes=64, name="xri")
                cs = slice(k * IL_COLS, (k + 1) * IL_COLS)
                nblk = D // IL_COLS
                eng = nc.vector.tensor_copy if k >= nblk - IL_V else nc.scalar.copy
                interleave(eng, xri[i][:, cs, :], xrs[i][:, :, cs])

            def quant_xr(i):
                xrq[i] = codes(D, "xrq%d" % i)
                quant(xrq[i], xri[i][:].rearrange("p d t -> p (d t)"))

            def scale_e(i, ts=range(T)):
                if i not in ebf:
                    ebf[i] = work.tile([P, T, O], BF16, tag="ebf", bufs=2, align_bytes=64, name="ebf")
                sl = slice(ts[0] * O, (ts[-1] + 1) * O)
                nc.vector.tensor_tensor(
                    out=ebf[i][:].rearrange("p t o -> p (t o)")[:, sl],
                    in0=ebs[i][:, sl].bitcast(FP8),
                    in1=es[:].rearrange("p t o -> p (t o)")[:, sl],
                    op=MULT,
                )

            def transposes(words, t2, key, off):
                b = psum.tile([P, 2, 2 * P], F32, tag="tr", bufs=TR, name="tr")
                for a in range(2):
                    for u in range(2):
                        nc.tensor.transpose(b[:, u, a * P : (a + 1) * P], words(2 * t2 + a)[:, off + u : off + 2 * P : 2], ident[:])
                bank[key] = b

            def tr_x(i, k):
                c, t2 = k // 2, k % 2
                transposes(lambda t: xs[i][:, t, :].bitcast(F32), t2, ("x", i, k), 256 * c)

            def exit_x(i, k):
                c, t2 = k // 2, k % 2
                if (i, c) not in xt:
                    xt[i, c] = work.tile([P, T * P * 4], BF16, tag="xt", bufs=3, align_bytes=64, name="xt")
                b = bank[("x", i, k)]
                nc.vector.tensor_tensor(
                    out=xt[i, c][:, t2 * 1024 : (t2 + 1) * 1024].rearrange("p (m u e) -> p m u e", u=2, e=2),
                    in0=b[:].bitcast(BF16).rearrange("p u (m e) -> p m u e", e=2),
                    in1=p_sb[:, c : c + 1, :].rearrange("p o (u e) -> p o u e", u=2).to_broadcast([P, 256, 2, 2]),
                    op=MULT,
                )

            def quant_part(cs, src, part, parts):
                n = src.shape[1] // parts
                ws = slice(part * n // 4, (part + 1) * n // 4)
                nc.vector.quantize_mx(out=cs[0][:, ws].bitcast(FP8X4), scales=cs[1][:, ws], in_=src[:, part * n : (part + 1) * n])

            def quant_x(i, c, part=0, parts=1):
                if (i, c) not in xq:
                    xq[i, c] = codes_w(T * P, "xq", 4)
                quant_part(xq[i, c], xt[i, c][:], part, parts)

            def tr_e(i, t2):
                transposes(lambda t: ebf[i][:, t, :].bitcast(F32), t2, ("e", i, t2), 0)

            def exit_e(i, t2):
                if i not in et:
                    et[i] = work.tile([P, T * P * 4], BF16, tag="et", bufs=2, align_bytes=64, name="et")
                b = bank[("e", i, t2)]
                nc.scalar.copy(
                    out=et[i][:, t2 * 1024 : (t2 + 1) * 1024].bitcast(F32).rearrange("p (m u) -> p m u", u=2),
                    in_=b[:].rearrange("p u m -> p m u"),
                )

            def quant_e(i, part=0, parts=1):
                if i not in eq:
                    eq[i] = codes_w(T * P, "eq", 2)
                quant_part(eq[i], et[i][:], part, parts)

            def mx(o, l, r_, cols, start, stop):
                nc.tensor.matmul_mx(
                    out=o,
                    lhsT=l[0][:, cols].bitcast(FP8X4),
                    lhsT_scale=l[1][:, cols],
                    rhs=r_[0][:].bitcast(FP8X4),
                    rhs_scale=r_[1][:],
                    start=start,
                    stop=stop,
                )

            def mm_u(i, t, s):
                b = psum.tile([P, H], F32, tag="u", bufs=UB, name="u")
                cols = slice(t * P, (t + 1) * P)
                mx(b[:], xq[i, 0], w1q[0], cols, True, False)
                mx(b[:], xq[i, 1], w1q[1], cols, False, False)
                mx(b[:], eq[i], w2q[s], cols, False, True)
                bank[("u", i, t, s)] = b

            def tanh(i, t, s):
                if (i, t // 2, s) not in hps:
                    hps[i, t // 2, s] = work.tile([P, 2, H], F32, tag="h%d" % s, bufs=2, align_bytes=64, name="h%d" % s)
                nc.scalar.activation(out=hps[i, t // 2, s][:, t % 2, :], in_=bank[("u", i, t, s)][:], func=TANH)

            def diff(i, t):
                if i in SG:
                    if t == 0:
                        dsc[i] = work.tile([P, T, H], BF16, tag="dif", bufs=2, align_bytes=64, name="dsc")
                    nc.vector.scalar_tensor_tensor(out=dsc[i][:, t, :], in0=hps[i, t // 2, 0][:, t % 2, :], scalar=g64[:, i, t : t + 1], in1=hps[i, t // 2, 1][:, t % 2, :], op0=MULT, op1=SUB)
                    return
                if i not in dif:
                    dif[i] = work.tile([P, T, H], F32, tag="dif", bufs=2, align_bytes=64, name="dif")
                if t % 2 == 1:
                    nc.vector.tensor_tensor(out=dif[i][:, t - 1 : t + 1, :], in0=hps[i, t // 2, 0][:], in1=hps[i, t // 2, 1][:], op=SUB)

            def gmul(i, h):
                if i not in dil:
                    dil[i] = work.tile([P, H, T], BF16, tag="dil", bufs=2, align_bytes=64, name="dil")
                hs = slice(h * 256, (h + 1) * 256)
                nc.vector.tensor_tensor(
                    out=dil[i][:, hs, :],
                    in0=dif[i][:, :, hs].rearrange("p t h -> p h t"),
                    in1=g64[:, i : i + 1, :].to_broadcast([P, 256, T]),
                    op=MULT,
                )

            def quant_d(i, part=0, parts=1):
                if i not in dq:
                    dq[i] = codes(H, "dq%d" % i)
                quant_part(dq[i], dil[i][:].rearrange("p h t -> p (h t)"), part, parts)

            def gscale(i, t):
                h = hps[i, t // 2, 1][:, t % 2, :]
                nc.scalar.activation(out=h, in_=h, func=mybir.ActivationFunctionType.Copy, scale=g64[:, i, t : t + 1])

            def gil(i, h):
                if i not in dil:
                    dil[i] = work.tile([P, H, T], BF16, tag="dil", bufs=2, align_bytes=64, name="dil")
                hs = slice(h * 256, (h + 1) * 256)
                interleave(nc.vector.tensor_copy, dil[i][:, hs, :], dsc[i][:, :, hs])

            def mm_acc(i, m, tag=None):
                if m not in acc:
                    if m < OPEN:
                        acc[m] = psum.tile([P, H], F32, tag="acc%d" % m, bufs=1, name="acc")
                    elif m < OPEN + TR:
                        acc[m] = psum.tile([P, H], F32, tag="tr", bufs=TR, name="tr")
                    else:
                        acc[m] = psum.tile([P, H], F32, tag="u", bufs=UB, name="u")
                mx(acc[m][:], xrq[i], dq[i], slice(m * P, (m + 1) * P), i == first.get(m, 0), i == G - 1)

            part = {}
            outs = []

            def chunk(m, k0):
                b = psum.tile([P, H], F32, tag="u", bufs=UB, name="u")
                for k in range(k0):
                    mx(b[:], xrq[k], dq[k], slice(m * P, (m + 1) * P), k == 0, k == k0 - 1)
                part[m] = work.tile([P, H], F32, tag="part", bufs=5, name="part")
                nc.scalar.copy(out=part[m][:], in_=b[:])
                first[m] = k0

            first = {}

            def finish(m):
                if m % 4 == 0:
                    outs.append(work.tile([P, 4, H], F32, tag="xrs", bufs=2, align_bytes=64, name="o"))
                o = outs[m // 4][:, m % 4, :]
                if m in part:
                    nc.vector.tensor_tensor(out=o, in0=acc[m][:], in1=part[m][:], op=mybir.AluOpType.add)
                elif m % 2 == 0 or len(part) > 3:
                    nc.scalar.copy(out=o, in_=acc[m][:])
                else:
                    nc.vector.tensor_copy(out=o, in_=acc[m][:])
                nc.sync.dma_start(out=out[m * P : (m + 1) * P, :], in_=o)

            nblk = D // IL_COLS
            ilq = [(i, k) for i in range(G) for k in range(nblk)]
            ilpos = [0]

            def il_upto(pos):
                while ilpos[0] < min(pos, len(ilq)):
                    inter_xr(*ilq[ilpos[0]])
                    ilpos[0] += 1

            w2t = work.tile([P, T * P * 4], BF16, tag="ebf", bufs=2, align_bytes=64, name="w2t")
            w1i = [work.tile([P, H, T], BF16, tag="xri", bufs=2, align_bytes=64, name="w1i") for c in range(2)]

            def il_w1(eng, c, k):
                interleave(eng, w1i[c][:, k * 128 : (k + 1) * 128, :], w1_raw[c][:, :, k * 128 : (k + 1) * 128])

            w2h = [None, None]
            w2q = [None, None]

            def prep_w2(s):
                w2h[s] = w2t
                if s == 1:
                    w2h[s] = work.tile([P, T * P * 4], BF16, tag="dil", bufs=2, align_bytes=64, name="w2h")
                    nc.vector.tensor_scalar(out=w2h[s][:], in0=w2t[:], scalar1=-1.0, scalar2=None, op0=MULT)

            def quant_w2(s):
                w2q[s] = codes(H, "w2q%d" % s)
                quant(w2q[s], w2h[s][:])

            tr_x(0, 0)
            exit_x(0, 0)
            tr_x(0, 2)
            exit_x(0, 2)
            scale_e(0, range(0, 2))
            tr_e(0, 0)
            exit_e(0, 0)
            for t2 in range(2):
                transposes(lambda t: w2_raw[:, t, :].bitcast(F32), t2, ("w2", t2), 0)
                nc.scalar.copy(
                    out=w2t[:, t2 * 1024 : (t2 + 1) * 1024].bitcast(F32).rearrange("p (m u) -> p m u", u=2),
                    in_=bank[("w2", t2)][:].rearrange("p u m -> p m u"),
                )
            quant_e(0, 0, 2)
            quant_x(0, 0, 0, 2)
            quant_x(0, 1, 0, 2)
            scale_e(0, range(2, 4))
            prep_w2(0)
            prep_w2(1)
            for c in range(2):
                il_w1(nc.scalar.copy, c, 0)
                il_w1(nc.scalar.copy, c, 1)
                il_w1(nc.vector.tensor_copy, c, 2)
                il_w1(nc.vector.tensor_copy, c, 3)
            quant_w2(0)
            quant_w2(1)
            w1q = [codes(H, "w1q%d" % c) for c in range(2)]
            for c in range(2):
                quant(w1q[c], w1i[c][:].rearrange("p h t -> p (h t)"))
            tr_e(0, 1)
            exit_e(0, 1)
            tr_x(0, 1)
            tr_x(0, 3)
            scale_xr(0)
            exit_x(0, 1)
            exit_x(0, 3)
            quant_e(0, 1, 2)
            quant_x(0, 0, 1, 2)
            quant_x(0, 1, 1, 2)
            scale_e(1)

            def gm(i, h):
                if i in SG:
                    gil(i, h)
                else:
                    gmul(i, h)

            dpos = [0]

            def diffs_upto(pos):
                while dpos[0] < pos:
                    diff(dpos[0] // T, dpos[0] % T)
                    dpos[0] += 1

            tr_x(1, 0)
            tr_x(1, 1)
            for i in range(G):
                n = i + 1
                pr = i - 1
                if i + 3 < G:
                    load_x(i + 3)
                    load_e(i + 3)
                for t in range(T):
                    sides = (1, 0) if i in SG else (0, 1)
                    for s in sides:
                        mm_u(i, t, s)
                    if (i, t) in CH:
                        chunk(*CH[i, t])
                    if n < G:
                        if t == 0:
                            exit_x(n, 0)
                            exit_x(n, 1)
                        elif t == 1:
                            exit_x(n, 2)
                            exit_x(n, 3)
                        elif t == 2:
                            exit_e(n, 0)
                            exit_e(n, 1)
                        if t == 0:
                            tr_x(n, 2)
                            tr_x(n, 3)
                        elif t == 1:
                            tr_e(n, 0)
                            tr_e(n, 1)
                        elif t == 3 and n + 1 < G:
                            tr_x(n + 1, 0)
                            tr_x(n + 1, 1)
                    pos = 8 * i + 2 * t + SHIFT
                    tanh(i, t, sides[0])
                    if i in SG:
                        gscale(i, t)
                    il_upto(pos + 1)
                    tanh(i, t, sides[1])
                    il_upto(pos + 2)
                    if t == QX:
                        for q in range(n):
                            if q not in xrq and ilpos[0] - QD >= 8 * (q + 1):
                                quant_xr(q)
                    lag = LAG if n < G else LAG7
                    dp = 4 * i + t - lag + 1
                    if t == 0:
                        if n < G:
                            scale_xr(n)
                        diffs_upto(dp)
                    elif t == 1:
                        if n < G:
                            quant_x(n, 0)
                        diffs_upto(dp)
                    elif t == 2:
                        if pr >= 0:
                            gm(pr, 0)
                        if n < G:
                            quant_x(n, 1)
                        if pr >= 0:
                            gm(pr, 1)
                        diffs_upto(dp)
                    else:
                        if n < G:
                            quant_e(n)
                        if pr >= 0:
                            quant_d(pr)
                        if n + 1 < G:
                            scale_e(n + 1)
                        diffs_upto(dp)
                        if pr >= 0:
                            for m in range(OPEN):
                                mm_acc(pr, m)
            last = G - 1
            if last not in xrq:
                quant_xr(last)
            for m in range(OPEN, 8):
                for k in range(7):
                    if k >= first.get(m, 0):
                        mm_acc(k, m)
            diffs_upto(4 * G)
            for h in range(2):
                gm(last, h)
                quant_d(last, h, 2)
            for m in range(8):
                mm_acc(last, m)
                finish(m)
